import numpy as np
import ml_dtypes

BF16 = ml_dtypes.bfloat16


def bf(x):
    return np.asarray(x, np.float32).astype(BF16)


def f32(x):
    return np.asarray(x, np.float32)


def f64(x):
    return np.asarray(x).astype(np.float64)


def striped(idx):
    return np.tile(idx.reshape(-1, 16).T, (8, 1))


S, K, M, N, E, Q, O = 512, 256, 128, 512, 4, 128, 128


def setup_inputs():
    return {"base": bf(np.random.standard_normal((M, S))), "x": bf(np.random.standard_normal((K, N))), "w": bf(1.2 * np.random.standard_normal((E, K, M)) / np.sqrt(K)), "w2": bf(np.random.standard_normal((M, O)) / np.sqrt(2 * M)), "b": f32(0.5 * np.random.standard_normal((O, 1))), "offs": striped(np.random.permutation(S))}


def reference(base, x, w, w2, b, offs):
    idx = offs[:16].T.reshape(-1)
    z = f64(base).copy()
    for e in range(E):
        z[:, idx[e * Q : (e + 1) * Q]] += f64(w)[e].T @ f64(x)[:, e * Q : (e + 1) * Q]
    y = f64(w2).T @ z
    return y + f64(b)

@@ -1,0 +1,62 @@
+import concourse.mybir as mybir
+from concourse.masks import make_identity
+
+BF16, F32, U16 = mybir.dt.bfloat16, mybir.dt.float32, mybir.dt.uint16
+IDENTITY = mybir.ActivationFunctionType.Identity
+
+FLOPS = 2 * 256 * 128 * 512 + 2 * 128 * 128 * 512
+
+
+def tile_rows_thenproj_bias_kernel(tc, base, x, w, w2, b, offs, out):
+    nc = tc.nc
+    M, S = base.shape
+    K, N = x.shape
+    E = w.shape[0]
+    O = w2.shape[1]
+    P = 128
+    C = K // P
+    Q = N // E
+    G = Q // 16
+    H = S // 2
+
+    with (
+        tc.tile_pool(name="held", bufs=1) as held,
+        tc.psum_pool(name="psum", bufs=1) as psum,
+    ):
+        base_t = held.tile([P, S], BF16)
+        offsets = held.tile([P, N // 16], U16)
+        w_t = held.tile([P, E, C, M], BF16)
+        x_t = held.tile([P, C, N], BF16)
+        w2_t = held.tile([P, O], BF16)
+        b_t = held.tile([P, 1], F32)
+
+        nc.sync.dma_start(base_t[:], base)
+        nc.sync.dma_start(offsets[:], offs)
+        nc.scalar.dma_start(x_t[:], x.rearrange("(p c) n -> p c n", c=C))
+        nc.sync.dma_start(w_t[:], w.rearrange("e (p c) m -> p e c m", c=C))
+        nc.scalar.dma_start(w2_t[:], w2)
+        nc.scalar.dma_start(b_t[:], b)
+
+        ident = held.tile([P, P], BF16)
+        make_identity(nc, ident[:])
+
+        window = psum.tile([P, S], F32)
+        nc.tensor.matmul(window[:], ident[:], base_t[:], start=True, stop=False)
+
+        for e in range(E):
+            places = window[:].indirect(offsets[:, e * G : (e + 1) * G])
+            for c in range(C):
+                last = e == E - 1 and c == C - 1
+                nc.tensor.matmul(places, w_t[:, e, c, :], x_t[:, c, e * Q : (e + 1) * Q], start=False, stop=last)
+
+        z_t = held.tile([P, S], BF16)
+        for h in range(2):
+            nc.vector.tensor_copy(z_t[:, h * H : (h + 1) * H], window[:, h * H : (h + 1) * H])
+        y = [psum.tile([P, H], F32, name=f"y{h}") for h in range(2)]
+        for h in range(2):
+            nc.tensor.matmul(y[h][:], w2_t[:], z_t[:, h * H : (h + 1) * H], start=True, stop=True)
+        out_t = [held.tile([P, H], F32, name=f"out{h}") for h in range(2)]
+        nc.scalar.activation(out_t[0][:], y[0][:], IDENTITY, bias=b_t[:])
+        nc.vector.tensor_scalar_add(out_t[1][:], y[1][:], b_t[:])
+        nc.scalar.dma_start(out[:, :H], out_t[0][:])
+        nc.sync.dma_start(out[:, H:], out_t[1][:])

@@ -4,6 +4,8 @@ from concourse.masks import make_identity
 BF16, F32, U16 = mybir.dt.bfloat16, mybir.dt.float32, mybir.dt.uint16
 IDENTITY = mybir.ActivationFunctionType.Identity
 
+WARM_UPS = 5
+
 FLOPS = 2 * 256 * 128 * 512 + 2 * 128 * 128 * 512
 
 
@@ -37,6 +39,15 @@ def tile_rows_thenproj_bias_kernel(tc, base, x, w, w2, b, offs, out):
         nc.scalar.dma_start(w2_t[:], w2)
         nc.scalar.dma_start(b_t[:], b)
 
+        zeros = held.tile([P, S], BF16)
+        nc.vector.memset(zeros[:], 0.0)
+        warm = psum.tile([P, S], F32)
+        for i in range(WARM_UPS):
+            nc.tensor.matmul(warm[:], zeros[:, :P], zeros[:], start=True, stop=True)
+
+        unread = held.tile([P, 1], F32)
+        nc.scalar.activation(unread[:], zeros[:, :1], IDENTITY)
+
         ident = held.tile([P, P], BF16)
         make_identity(nc, ident[:])
 
@@ -52,11 +63,11 @@ def tile_rows_thenproj_bias_kernel(tc, base, x, w, w2, b, offs, out):
         z_t = held.tile([P, S], BF16)
         for h in range(2):
             nc.vector.tensor_copy(z_t[:, h * H : (h + 1) * H], window[:, h * H : (h + 1) * H])
-        y = [psum.tile([P, H], F32, name=f"y{h}") for h in range(2)]
+        y = [psum.tile([P, S], F32, name=f"y{h}")[:, :H] for h in range(2)]
         for h in range(2):
-            nc.tensor.matmul(y[h][:], w2_t[:], z_t[:, h * H : (h + 1) * H], start=True, stop=True)
+            nc.tensor.matmul(y[h], w2_t[:], z_t[:, h * H : (h + 1) * H], start=True, stop=True)
         out_t = [held.tile([P, H], F32, name=f"out{h}") for h in range(2)]
-        nc.scalar.activation(out_t[0][:], y[0][:], IDENTITY, bias=b_t[:])
-        nc.vector.tensor_scalar_add(out_t[1][:], y[1][:], b_t[:])
+        nc.scalar.activation(out_t[0][:], y[0], IDENTITY, bias=b_t[:])
+        nc.vector.tensor_scalar_add(out_t[1][:], y[1], b_t[:])
         nc.scalar.dma_start(out[:, :H], out_t[0][:])
         nc.sync.dma_start(out[:, H:], out_t[1][:])

import concourse.mybir as mybir
from concourse.masks import make_identity

BF16, F32, U16 = mybir.dt.bfloat16, mybir.dt.float32, mybir.dt.uint16
IDENTITY = mybir.ActivationFunctionType.Identity

WARM_UPS = 5

FLOPS = 2 * 256 * 128 * 512 + 2 * 128 * 128 * 512


def tile_rows_thenproj_bias_kernel(tc, base, x, w, w2, b, offs, out):
    nc = tc.nc
    M, S = base.shape
    K, N = x.shape
    E = w.shape[0]
    O = w2.shape[1]
    P = 128
    C = K // P
    Q = N // E
    G = Q // 16
    H = S // 2

    with (
        tc.tile_pool(name="held", bufs=1) as held,
        tc.psum_pool(name="psum", bufs=1) as psum,
    ):
        base_t = held.tile([P, S], BF16)
        offsets = held.tile([P, N // 16], U16)
        w_t = held.tile([P, E, C, M], BF16)
        x_t = held.tile([P, C, N], BF16)
        w2_t = held.tile([P, O], BF16)
        b_t = held.tile([P, 1], F32)

        nc.sync.dma_start(base_t[:], base)
        nc.sync.dma_start(offsets[:], offs)
        nc.scalar.dma_start(x_t[:], x.rearrange("(p c) n -> p c n", c=C))
        nc.sync.dma_start(w_t[:], w.rearrange("e (p c) m -> p e c m", c=C))
        nc.scalar.dma_start(w2_t[:], w2)
        nc.scalar.dma_start(b_t[:], b)

        zeros = held.tile([P, S], BF16)
        nc.vector.memset(zeros[:], 0.0)
        warm = psum.tile([P, S], F32)
        for i in range(WARM_UPS):
            nc.tensor.matmul(warm[:], zeros[:, :P], zeros[:], start=True, stop=True)

        unread = held.tile([P, 1], F32)
        nc.scalar.activation(unread[:], zeros[:, :1], IDENTITY)

        ident = held.tile([P, P], BF16)
        make_identity(nc, ident[:])

        window = psum.tile([P, S], F32)
        nc.tensor.matmul(window[:], ident[:], base_t[:], start=True, stop=False)

        for e in range(E):
            places = window[:].indirect(offsets[:, e * G : (e + 1) * G])
            for c in range(C):
                last = e == E - 1 and c == C - 1
                nc.tensor.matmul(places, w_t[:, e, c, :], x_t[:, c, e * Q : (e + 1) * Q], start=False, stop=last)

        z_t = held.tile([P, S], BF16)
        for h in range(2):
            nc.vector.tensor_copy(z_t[:, h * H : (h + 1) * H], window[:, h * H : (h + 1) * H])
        y = [psum.tile([P, S], F32, name=f"y{h}")[:, :H] for h in range(2)]
        for h in range(2):
            nc.tensor.matmul(y[h], w2_t[:], z_t[:, h * H : (h + 1) * H], start=True, stop=True)
        out_t = [held.tile([P, H], F32, name=f"out{h}") for h in range(2)]
        nc.scalar.activation(out_t[0][:], y[0], IDENTITY, bias=b_t[:])
        nc.vector.tensor_scalar_add(out_t[1][:], y[1], b_t[:])
        nc.scalar.dma_start(out[:, :H], out_t[0][:])
        nc.sync.dma_start(out[:, H:], out_t[1][:])
